import numpy as np
import ml_dtypes


def mxq(x, axis, fmt="e4m3"):
    dtype, down = {"e4m3": (ml_dtypes.float8_e4m3fn, 7), "e5m2": (ml_dtypes.float8_e5m2, 14)}[fmt]
    v = np.moveaxis(np.asarray(x, np.float32).astype(ml_dtypes.bfloat16).astype(np.float64), axis, -1)
    blocks = v.reshape(v.shape[:-1] + (-1, 32))
    amax = np.abs(blocks).max(-1, keepdims=True)
    byte = np.maximum(np.where(amax > 0, np.frexp(amax)[1] - 1 + 127, 0) - down, 1)
    scale = np.exp2(byte - 127.0)
    codes = (blocks / scale).astype(np.float32).astype(dtype).astype(np.float64)
    return np.moveaxis((codes * scale).reshape(v.shape), -1, axis)


WIDE = False


def mx_kscale(k):
    if not WIDE:
        return np.ones(k)
    levels = np.array([30, -30])
    if k % 512:
        return np.exp2(np.random.permutation(np.resize(levels, k // 32))).repeat(32)
    a = np.empty((k // 512, 16))
    for p in range(k // 512):
        a[p, :8] = np.random.permutation(np.resize(levels, 8))
        for g in range(8):
            far = levels[np.abs(levels - a[p, g]) >= 10]
            a[p, g + 8] = far[np.random.randint(len(far))]
    return np.exp2(a.ravel()).repeat(32)


def f64(x):
    return np.asarray(x).astype(np.float64)


def striped(idx):
    return np.tile(np.asarray(idx).reshape(-1, 16).T, (8, 1)).astype(np.uint16)


def unstriped(offs):
    return offs[:16].T.reshape(-1).astype(np.int64)


E2M1 = np.array([0.0, 0.5, 1.0, 1.5, 2.0, 3.0, 4.0, 6.0, -0.0, -0.5, -1.0, -1.5, -2.0, -3.0, -4.0, -6.0])


def pack_weight(w, fmt):
    k, n = w.shape
    w = f64(np.asarray(w, np.float32).astype(ml_dtypes.bfloat16)).reshape(k // 32, 32, n)
    amax = np.abs(w).max(1)
    if fmt in ("e4m3", "e5m2"):
        byte = np.frexp(amax)[1] - 1 + 127 - (7 if fmt == "e4m3" else 14)
    else:
        mant, ex = np.frexp(amax / 6.0)
        byte = np.where(mant > 0.5, ex, ex - 1) + 127
    byte = np.clip(np.where(amax > 0, byte, 1), 1, 254)
    scaled = (w * np.exp2(127.0 - byte)[:, None, :]).reshape(k, n).astype(np.float32)
    by_word = np.ascontiguousarray(scaled.reshape(k // 512, 128, 4, n).transpose(0, 1, 3, 2))
    if fmt in ("e4m3", "e5m2"):
        words = by_word.astype(ml_dtypes.float8_e4m3fn if fmt == "e4m3" else ml_dtypes.float8_e5m2).view(np.uint8)
    else:
        c = by_word.astype(ml_dtypes.float4_e2m1fn).view(np.uint8) & 0xF
        words = (c[..., 0::2] | (c[..., 1::2] << 4)).reshape(k // 512, 128, 2 * n)
    return np.ascontiguousarray(words), np.ascontiguousarray(byte.astype(np.uint8).reshape(k // 512, 16, n))


def unpack_weight(words, scales, fmt):
    g, _, n = scales.shape
    words = np.ascontiguousarray(words).reshape(g, 128, n, -1)
    if fmt in ("e4m3", "e5m2"):
        vals = words.view(ml_dtypes.float8_e4m3fn if fmt == "e4m3" else ml_dtypes.float8_e5m2).astype(np.float64)
    else:
        nib = np.empty((g, 128, n, 4), np.uint8)
        nib[..., 0::2] = words & 0xF
        nib[..., 1::2] = words >> 4
        vals = E2M1[nib]
    vals = vals * np.repeat(np.exp2(scales.astype(np.float64) - 127.0), 8, axis=1)[..., None]
    return vals.transpose(0, 1, 3, 2).reshape(g * 512, n)


K, T, J, N, L, G = 1024, 1024, 256, 256, 512, 32


def setup_inputs():
    n = np.random.standard_normal
    idx = np.random.permutation(T)[:J]
    fk = mx_kscale(K)
    fl = mx_kscale(L)
    xtp = pack_weight(n((K, T)) * np.random.uniform(0.4, 1.6, (1, T)) / fk[:, None], "e4m3")
    wap = pack_weight(n((K, N)) * 1 / np.sqrt(K) * fk[:, None], "e5m2")
    wbp = pack_weight(n((L, N)) * 1 / np.sqrt(L) * fl[:, None], "e5m2")
    return {
        "xt_words": xtp[0],
        "xt_scales": xtp[1],
        "wa_words": wap[0],
        "wa_scales": wap[1],
        "sx": (n((L, J)) * np.random.uniform(0.4, 1.6, (1, J)) / fl[:, None]).astype(np.float32),
        "wb_words": wbp[0],
        "wb_scales": wbp[1],
        "bi": (np.random.uniform(-0.6, 0.6, (1, N))).astype(np.float32),
        "offs": striped(idx),
    }


def reference(xt_words, xt_scales, wa_words, wa_scales, sx, wb_words, wb_scales, bi, offs):
    idx = unstriped(offs)
    xtu = unpack_weight(xt_words, xt_scales, "e4m3")
    wau = unpack_weight(wa_words, wa_scales, "e5m2")
    wbu = unpack_weight(wb_words, wb_scales, "e5m2")
    xtidxg = xtu[:, idx]
    a = xtidxg.T @ wau
    sxq = mxq(f64(sx), 0, "e5m2")
    b0 = sxq.T @ wbu
    b2 = b0 + f64(bi)
    g1 = a.reshape(J, G, N // G).max(axis=2)
    g2 = b2.reshape(J, G, N // G).mean(axis=2)
    y = g1 - 1.5 * g2
    return y

@@ -1,0 +1,166 @@
+from contextlib import ExitStack
+
+import concourse.mybir as mybir
+from concourse.masks import make_identity
+
+K, T, J, N, L, G = 1024, 1024, 256, 256, 512, 32
+FLOPS = 2 * J * N * (K + L)
+
+F32 = mybir.dt.float32
+BF16 = mybir.dt.bfloat16
+I32 = mybir.dt.int32
+U32 = mybir.dt.uint32
+U16 = mybir.dt.uint16
+U8 = mybir.dt.uint8
+E4M3 = mybir.dt.float8_e4m3fn_x4
+E5M2 = mybir.dt.float8_e5m2_x4
+ALU = mybir.AluOpType
+AX = mybir.AxisListType.X
+
+P = 128
+SET = N // G
+PASSES = K // 512
+HALVES = J // P
+
+
+def load_scale_rows(queue, plane, scales):
+    passes = scales.shape[0]
+    rows = scales.rearrange("z (q r) c -> r q z c", r=4)
+    for r in range(4):
+        queue.dma_start(
+            out=plane[r:P:32, :].bitcast(I32).rearrange("q (z c) -> q z c", z=passes),
+            in_=rows[r].bitcast(I32),
+        )
+
+
+def tile_list_rows_owninput_peakofgroups_kernel(
+    tc, xt_words, xt_scales, wa_words, wa_scales, sx, wb_words, wb_scales, bi, offs, out
+):
+    nc = tc.nc
+    with ExitStack() as ctx:
+        sb = ctx.enter_context(tc.tile_pool(name="sb", bufs=1))
+        ps = ctx.enter_context(tc.psum_pool(name="ps", bufs=1))
+
+        offsets = sb.tile([P, J // 16], U16, name="offsets")
+        xs = sb.tile([P, PASSES * T], U8, name="xs", align_bytes=64)
+        xw = [sb.tile([P, T], I32, name="xw%d" % z, align_bytes=64) for z in range(PASSES)]
+        sx_raw = sb.tile([P, 4, J], F32, name="sx_raw", align_bytes=64)
+        wa_w = sb.tile([P, PASSES, N], I32, name="wa_w", align_bytes=64)
+        wa_s = sb.tile([P, PASSES * N], U8, name="wa_s", align_bytes=64)
+        wb_w = sb.tile([P, N], I32, name="wb_w", align_bytes=64)
+        wb_s = sb.tile([P, N], U8, name="wb_s", align_bytes=64)
+        bias = sb.tile([P, SET], F32, name="bias")
+        ident = sb.tile([P, P], F32, name="ident")
+
+        nc.vector.memset(xs[:].bitcast(I32), 0)
+        nc.vector.memset(wb_s[:].bitcast(I32), 0)
+        nc.vector.memset(wa_s[:].bitcast(I32), 0)
+        nc.vector.memset(bias[:], 0.0)
+
+        nc.sync.dma_start(offsets[:], offs)
+        load_scale_rows(nc.scalar, xs, xt_scales)
+        nc.sync.dma_start(out=sx_raw[:], in_=sx.rearrange("(p t) j -> p t j", t=4))
+        for z in range(PASSES):
+            nc.sync.dma_start(out=xw[z][:], in_=xt_words[z].rearrange("p c t -> p (c t)").bitcast(I32))
+        load_scale_rows(nc.gpsimd, wb_s, wb_scales)
+        nc.sync.dma_start(out=bias[0:G, :], in_=bi.rearrange("o (g r) -> (o g) r", r=SET))
+        nc.sync.dma_start(out=wb_w[:], in_=wb_words[0].rearrange("p c t -> p (c t)").bitcast(I32))
+        nc.sync.dma_start(out=wa_w[:], in_=wa_words.rearrange("z p c t -> p z (c t)").bitcast(I32))
+        load_scale_rows(nc.sync, wa_s, wa_scales)
+        make_identity(nc, ident[:])
+
+        gs = [sb.tile([P, J], U8, name="gs%d" % z, align_bytes=64) for z in range(PASSES)]
+        gw = [sb.tile([P, J], U32, name="gw%d" % z, align_bytes=64) for z in range(PASSES)]
+        for z in range(PASSES):
+            nc.vector.tensor_copy(gs[z][:], xs[:, z * T : (z + 1) * T].indirect(offsets[:]))
+
+        sx_bf = sb.tile([P, J, 4], BF16, name="sx_bf", align_bytes=64)
+        nc.scalar.copy(
+            out=sx_bf[:].rearrange("p (c i) t -> p c t i", i=4),
+            in_=sx_raw[:].rearrange("p t (c i) -> p c t i", i=4),
+        )
+
+        nc.vector.tensor_copy(gw[0][:], xw[0][:].bitcast(U32).indirect(offsets[:]))
+
+        sx_w = sb.tile([P, J], U32, name="sx_w", align_bytes=64)
+        sx_s = sb.tile([P, J], U8, name="sx_s", align_bytes=64)
+        nc.vector.quantize_mx(
+            out=sx_w[:].bitcast(E5M2), scales=sx_s[:], in_=sx_bf[:].rearrange("p j t -> p (j t)")
+        )
+
+        nc.vector.tensor_copy(gw[1][:], xw[1][:].bitcast(U32).indirect(offsets[:]))
+
+        bias_ps = ps.tile([P, P], F32, name="bias_ps")
+        for r in range(SET):
+            nc.tensor.matmul(
+                out=bias_ps[:],
+                lhsT=bias[:, r : r + 1].to_broadcast([P, P]),
+                rhs=ident[:],
+                is_transpose=True,
+                start=(r == 0),
+                stop=(r == SET - 1),
+            )
+
+        b_ps = ps.tile([P, HALVES, N], F32, name="b_ps")
+        for h in range(HALVES):
+            cols = slice(h * P, (h + 1) * P)
+            nc.tensor.matmul_mx(
+                out=b_ps[:, h, :],
+                lhsT=sx_w[:, cols].bitcast(E5M2),
+                lhsT_scale=sx_s[:, cols],
+                rhs=wb_w[:].bitcast(E5M2),
+                rhs_scale=wb_s[:],
+                start=True,
+                stop=True,
+            )
+
+        a_ps = [ps.tile([P, N], F32, name="a_ps%d" % h) for h in range(HALVES)]
+        for z in range(PASSES):
+            for h in range(HALVES):
+                cols = slice(h * P, (h + 1) * P)
+                nc.tensor.matmul_mx(
+                    out=a_ps[h][:],
+                    lhsT=gw[z][:, cols].bitcast(E4M3),
+                    lhsT_scale=gs[z][:, cols],
+                    rhs=wa_w[:, z, :].bitcast(E5M2),
+                    rhs_scale=wa_s[:, z * N : (z + 1) * N],
+                    start=(z == 0),
+                    stop=(z == PASSES - 1),
+                )
+
+        b_sum = sb.tile([P, HALVES, G], F32, name="b_sum")
+        nc.vector.tensor_reduce(
+            out=b_sum[:].rearrange("p h g -> p (h g)"),
+            in_=b_ps[:].rearrange("p h (g r) -> p (h g) r", r=SET),
+            axis=AX,
+            op=ALU.add,
+        )
+        b2_sum = sb.tile([P, HALVES, G], F32, name="b2_sum")
+        nc.vector.tensor_tensor(
+            out=b2_sum[:],
+            in0=b_sum[:],
+            in1=bias_ps[:, 0:G].unsqueeze(1).to_broadcast([P, HALVES, G]),
+            op=ALU.add,
+        )
+
+        peak = sb.tile([P, HALVES, G], F32, name="peak")
+        for h in range(HALVES):
+            nc.vector.tensor_reduce(
+                out=peak[:, h, :],
+                in_=a_ps[h][:].rearrange("p (g r) -> p g r", r=SET),
+                axis=AX,
+                op=ALU.max,
+            )
+        res = sb.tile([P, HALVES * G], F32, name="res")
+        nc.vector.scalar_tensor_tensor(
+            out=res[:],
+            in0=b2_sum[:].rearrange("p h g -> p (h g)"),
+            scalar=-1.5 / SET,
+            in1=peak[:].rearrange("p h g -> p (h g)"),
+            op0=ALU.mult,
+            op1=ALU.add,
+        )
+        nc.sync.dma_start(
+            out=out.rearrange("(h p) g -> p h g", p=P),
+            in_=res[:].rearrange("p (h g) -> p h g", g=G),
+        )

@@ -23,11 +23,11 @@ PASSES = K // 512
 HALVES = J // P
 
 
-def load_scale_rows(queue, plane, scales):
+def load_scale_rows(queues, plane, scales):
     passes = scales.shape[0]
     rows = scales.rearrange("z (q r) c -> r q z c", r=4)
     for r in range(4):
-        queue.dma_start(
+        queues[r].dma_start(
             out=plane[r:P:32, :].bitcast(I32).rearrange("q (z c) -> q z c", z=passes),
             in_=rows[r].bitcast(I32),
         )
@@ -49,25 +49,25 @@ def tile_list_rows_owninput_peakofgroups_kernel(
         wa_s = sb.tile([P, PASSES * N], U8, name="wa_s", align_bytes=64)
         wb_w = sb.tile([P, N], I32, name="wb_w", align_bytes=64)
         wb_s = sb.tile([P, N], U8, name="wb_s", align_bytes=64)
-        bias = sb.tile([P, SET], F32, name="bias")
+        bias = sb.tile([G, SET], F32, name="bias")
+        bias_sum = sb.tile([P, 1], F32, name="bias_sum")
         ident = sb.tile([P, P], F32, name="ident")
 
         nc.vector.memset(xs[:].bitcast(I32), 0)
-        nc.vector.memset(wb_s[:].bitcast(I32), 0)
-        nc.vector.memset(wa_s[:].bitcast(I32), 0)
-        nc.vector.memset(bias[:], 0.0)
+        nc.vector.memset(bias_sum[:], 0.0)
+        nc.vector.memset(ident[:], 0.0)
 
         nc.sync.dma_start(offsets[:], offs)
-        load_scale_rows(nc.scalar, xs, xt_scales)
         nc.sync.dma_start(out=sx_raw[:], in_=sx.rearrange("(p t) j -> p t j", t=4))
+        load_scale_rows([nc.sync] * 4, xs, xt_scales)
         for z in range(PASSES):
             nc.sync.dma_start(out=xw[z][:], in_=xt_words[z].rearrange("p c t -> p (c t)").bitcast(I32))
-        load_scale_rows(nc.gpsimd, wb_s, wb_scales)
-        nc.sync.dma_start(out=bias[0:G, :], in_=bi.rearrange("o (g r) -> (o g) r", r=SET))
         nc.sync.dma_start(out=wb_w[:], in_=wb_words[0].rearrange("p c t -> p (c t)").bitcast(I32))
+        load_scale_rows([nc.sync] * 4, wb_s, wb_scales)
         nc.sync.dma_start(out=wa_w[:], in_=wa_words.rearrange("z p c t -> p z (c t)").bitcast(I32))
-        load_scale_rows(nc.sync, wa_s, wa_scales)
-        make_identity(nc, ident[:])
+        nc.gpsimd.dma_start(out=bias[:], in_=bi.rearrange("o (g r) -> (o g) r", r=SET))
+        make_identity(nc, ident[:], nomemset=True)
+        load_scale_rows([nc.sync, nc.gpsimd, nc.gpsimd, nc.gpsimd], wa_s, wa_scales)
 
         gs = [sb.tile([P, J], U8, name="gs%d" % z, align_bytes=64) for z in range(PASSES)]
         gw = [sb.tile([P, J], U32, name="gw%d" % z, align_bytes=64) for z in range(PASSES)]
@@ -91,16 +91,6 @@ def tile_list_rows_owninput_peakofgroups_kernel(
         nc.vector.tensor_copy(gw[1][:], xw[1][:].bitcast(U32).indirect(offsets[:]))
 
         bias_ps = ps.tile([P, P], F32, name="bias_ps")
-        for r in range(SET):
-            nc.tensor.matmul(
-                out=bias_ps[:],
-                lhsT=bias[:, r : r + 1].to_broadcast([P, P]),
-                rhs=ident[:],
-                is_transpose=True,
-                start=(r == 0),
-                stop=(r == SET - 1),
-            )
-
         b_ps = ps.tile([P, HALVES, N], F32, name="b_ps")
         for h in range(HALVES):
             cols = slice(h * P, (h + 1) * P)
@@ -114,9 +104,12 @@ def tile_list_rows_owninput_peakofgroups_kernel(
                 stop=True,
             )
 
+        nc.scalar.activation(out=sx_raw[0:G, 0, 0:SET], in_=bias[:], func=mybir.ActivationFunctionType.Copy, accum_out=bias_sum[0:G, :])
+        nc.tensor.transpose(bias_ps[:], bias_sum[:].to_broadcast([P, P]), ident[:])
+
         a_ps = [ps.tile([P, N], F32, name="a_ps%d" % h) for h in range(HALVES)]
-        for z in range(PASSES):
-            for h in range(HALVES):
+        for h in range(HALVES):
+            for z in range(PASSES):
                 cols = slice(h * P, (h + 1) * P)
                 nc.tensor.matmul_mx(
                     out=a_ps[h][:],

@@ -15,22 +15,31 @@ U8 = mybir.dt.uint8
 E4M3 = mybir.dt.float8_e4m3fn_x4
 E5M2 = mybir.dt.float8_e5m2_x4
 ALU = mybir.AluOpType
-AX = mybir.AxisListType.X
+FREE_AXIS = mybir.AxisListType.X
 
 P = 128
+PACK = 4
+QUADRANT = 32
+ROWS = 4
+LIST_GROUP = 16
+ALIGN = 64
 SET = N // G
-PASSES = K // 512
+PASSES = K // (P * PACK)
 HALVES = J // P
 
 
-def load_scale_rows(queues, plane, scales):
+def load_scale_rows(queue, plane, scales, which):
     passes = scales.shape[0]
-    rows = scales.rearrange("z (q r) c -> r q z c", r=4)
-    for r in range(4):
-        queues[r].dma_start(
-            out=plane[r:P:32, :].bitcast(I32).rearrange("q (z c) -> q z c", z=passes),
+    rows = scales.rearrange("z (q r) c -> r q z c", r=ROWS)
+    for r in which:
+        queue.dma_start(
+            out=plane[r:P:QUADRANT, :].bitcast(I32).rearrange("q (z c) -> q z c", z=passes),
             in_=rows[r].bitcast(I32),
         )
+
+
+def words_by_partition(words):
+    return words.rearrange("z p c t -> p z (c t)").bitcast(I32)
 
 
 def tile_list_rows_owninput_peakofgroups_kernel(
@@ -41,119 +50,114 @@ def tile_list_rows_owninput_peakofgroups_kernel(
         sb = ctx.enter_context(tc.tile_pool(name="sb", bufs=1))
         ps = ctx.enter_context(tc.psum_pool(name="ps", bufs=1))
 
-        offsets = sb.tile([P, J // 16], U16, name="offsets")
-        xs = sb.tile([P, PASSES * T], U8, name="xs", align_bytes=64)
-        xw = [sb.tile([P, T], I32, name="xw%d" % z, align_bytes=64) for z in range(PASSES)]
-        sx_raw = sb.tile([P, 4, J], F32, name="sx_raw", align_bytes=64)
-        wa_w = sb.tile([P, PASSES, N], I32, name="wa_w", align_bytes=64)
-        wa_s = sb.tile([P, PASSES * N], U8, name="wa_s", align_bytes=64)
-        wb_w = sb.tile([P, N], I32, name="wb_w", align_bytes=64)
-        wb_s = sb.tile([P, N], U8, name="wb_s", align_bytes=64)
+        offsets = sb.tile([P, J // LIST_GROUP], U16, name="offsets")
+        xt_s = sb.tile([P, PASSES * T], U8, name="xt_s", align_bytes=ALIGN)
+        xt_w = sb.tile([P, PASSES, T], I32, name="xt_w", align_bytes=ALIGN)
+        sx_raw = sb.tile([P, PACK, J], F32, name="sx_raw", align_bytes=ALIGN)
+        wa_w = sb.tile([P, PASSES, N], I32, name="wa_w", align_bytes=ALIGN)
+        wa_s = sb.tile([P, PASSES * N], U8, name="wa_s", align_bytes=ALIGN)
+        wb_w = sb.tile([P, 1, N], I32, name="wb_w", align_bytes=ALIGN)
+        wb_s = sb.tile([P, N], U8, name="wb_s", align_bytes=ALIGN)
         bias = sb.tile([G, SET], F32, name="bias")
         bias_sum = sb.tile([P, 1], F32, name="bias_sum")
         ident = sb.tile([P, P], F32, name="ident")
 
-        nc.vector.memset(xs[:].bitcast(I32), 0)
+        nc.vector.memset(xt_s[:].bitcast(I32), 0)
         nc.vector.memset(bias_sum[:], 0.0)
         nc.vector.memset(ident[:], 0.0)
 
         nc.sync.dma_start(offsets[:], offs)
-        nc.sync.dma_start(out=sx_raw[:], in_=sx.rearrange("(p t) j -> p t j", t=4))
-        load_scale_rows([nc.sync] * 4, xs, xt_scales)
-        for z in range(PASSES):
-            nc.sync.dma_start(out=xw[z][:], in_=xt_words[z].rearrange("p c t -> p (c t)").bitcast(I32))
-        nc.sync.dma_start(out=wb_w[:], in_=wb_words[0].rearrange("p c t -> p (c t)").bitcast(I32))
-        load_scale_rows([nc.sync] * 4, wb_s, wb_scales)
-        nc.sync.dma_start(out=wa_w[:], in_=wa_words.rearrange("z p c t -> p z (c t)").bitcast(I32))
-        nc.gpsimd.dma_start(out=bias[:], in_=bi.rearrange("o (g r) -> (o g) r", r=SET))
+        nc.scalar.dma_start(out=bias[:], in_=bi.rearrange("o (g r) -> (o g) r", r=SET))
+        load_scale_rows(nc.gpsimd, wb_s, wb_scales, (2, 3))
+        load_scale_rows(nc.gpsimd, wa_s, wa_scales, (3,))
+        nc.sync.dma_start(out=sx_raw[:], in_=sx.rearrange("(p t) j -> p t j", t=PACK))
+        load_scale_rows(nc.sync, xt_s, xt_scales, range(ROWS))
+        nc.sync.dma_start(out=xt_w[:], in_=words_by_partition(xt_words))
+        load_scale_rows(nc.sync, wb_s, wb_scales, (0,))
+        nc.sync.dma_start(out=wb_w[:], in_=words_by_partition(wb_words))
+        load_scale_rows(nc.sync, wb_s, wb_scales, (1,))
+        nc.sync.dma_start(out=wa_w[:], in_=words_by_partition(wa_words))
+        load_scale_rows(nc.sync, wa_s, wa_scales, (0, 1, 2))
         make_identity(nc, ident[:], nomemset=True)
-        load_scale_rows([nc.sync, nc.gpsimd, nc.gpsimd, nc.gpsimd], wa_s, wa_scales)
 
-        gs = [sb.tile([P, J], U8, name="gs%d" % z, align_bytes=64) for z in range(PASSES)]
-        gw = [sb.tile([P, J], U32, name="gw%d" % z, align_bytes=64) for z in range(PASSES)]
+        nc.vector.tensor_reduce(out=bias_sum[0:G, :], in_=bias[:], axis=FREE_AXIS, op=ALU.add)
+        bias_ps = ps.tile([P, P], F32, name="bias_ps")
+        nc.tensor.transpose(bias_ps[:], bias_sum[:].to_broadcast([P, P]), ident[:])
+
+        picked_s = [sb.tile([P, J], U8, name="picked_s%d" % z, align_bytes=ALIGN) for z in range(PASSES)]
         for z in range(PASSES):
-            nc.vector.tensor_copy(gs[z][:], xs[:, z * T : (z + 1) * T].indirect(offsets[:]))
+            nc.vector.tensor_copy(picked_s[z][:], xt_s[:, z * T : (z + 1) * T].indirect(offsets[:]))
 
-        sx_bf = sb.tile([P, J, 4], BF16, name="sx_bf", align_bytes=64)
-        nc.scalar.copy(
-            out=sx_bf[:].rearrange("p (c i) t -> p c t i", i=4),
-            in_=sx_raw[:].rearrange("p t (c i) -> p c t i", i=4),
-        )
-
-        nc.vector.tensor_copy(gw[0][:], xw[0][:].bitcast(U32).indirect(offsets[:]))
-
-        sx_w = sb.tile([P, J], U32, name="sx_w", align_bytes=64)
-        sx_s = sb.tile([P, J], U8, name="sx_s", align_bytes=64)
+        sx_bf = sb.tile([P, J, PACK], BF16, name="sx_bf", align_bytes=ALIGN)
+        nc.scalar.copy(out=sx_bf[:], in_=sx_raw[:].rearrange("p t j -> p j t"))
+        sx_w = sb.tile([P, J], U32, name="sx_w", align_bytes=ALIGN)
+        sx_s = sb.tile([P, J], U8, name="sx_s", align_bytes=ALIGN)
         nc.vector.quantize_mx(
             out=sx_w[:].bitcast(E5M2), scales=sx_s[:], in_=sx_bf[:].rearrange("p j t -> p (j t)")
         )
 
-        nc.vector.tensor_copy(gw[1][:], xw[1][:].bitcast(U32).indirect(offsets[:]))
+        picked_w = [sb.tile([P, J], U32, name="picked_w%d" % z, align_bytes=ALIGN) for z in range(PASSES)]
+        for z in range(PASSES):
+            nc.vector.tensor_copy(picked_w[z][:], xt_w[:, z, :].bitcast(U32).indirect(offsets[:]))
 
-        bias_ps = ps.tile([P, P], F32, name="bias_ps")
         b_ps = ps.tile([P, HALVES, N], F32, name="b_ps")
         for h in range(HALVES):
-            cols = slice(h * P, (h + 1) * P)
+            slots = slice(h * P, (h + 1) * P)
             nc.tensor.matmul_mx(
                 out=b_ps[:, h, :],
-                lhsT=sx_w[:, cols].bitcast(E5M2),
-                lhsT_scale=sx_s[:, cols],
-                rhs=wb_w[:].bitcast(E5M2),
+                lhsT=sx_w[:, slots].bitcast(E5M2),
+                lhsT_scale=sx_s[:, slots],
+                rhs=wb_w[:, 0, :].bitcast(E5M2),
                 rhs_scale=wb_s[:],
                 start=True,
                 stop=True,
             )
 
-        nc.scalar.activation(out=sx_raw[0:G, 0, 0:SET], in_=bias[:], func=mybir.ActivationFunctionType.Copy, accum_out=bias_sum[0:G, :])
-        nc.tensor.transpose(bias_ps[:], bias_sum[:].to_broadcast([P, P]), ident[:])
-
         a_ps = [ps.tile([P, N], F32, name="a_ps%d" % h) for h in range(HALVES)]
         for h in range(HALVES):
+            slots = slice(h * P, (h + 1) * P)
             for z in range(PASSES):
-                cols = slice(h * P, (h + 1) * P)
                 nc.tensor.matmul_mx(
                     out=a_ps[h][:],
-                    lhsT=gw[z][:, cols].bitcast(E4M3),
-                    lhsT_scale=gs[z][:, cols],
+                    lhsT=picked_w[z][:, slots].bitcast(E4M3),
+                    lhsT_scale=picked_s[z][:, slots],
                     rhs=wa_w[:, z, :].bitcast(E5M2),
                     rhs_scale=wa_s[:, z * N : (z + 1) * N],
                     start=(z == 0),
                     stop=(z == PASSES - 1),
                 )
 
-        b_sum = sb.tile([P, HALVES, G], F32, name="b_sum")
+        b0_sum = sb.tile([P, HALVES, G], F32, name="b0_sum")
         nc.vector.tensor_reduce(
-            out=b_sum[:].rearrange("p h g -> p (h g)"),
+            out=b0_sum[:].rearrange("p h g -> p (h g)"),
             in_=b_ps[:].rearrange("p h (g r) -> p (h g) r", r=SET),
-            axis=AX,
+            axis=FREE_AXIS,
             op=ALU.add,
         )
         b2_sum = sb.tile([P, HALVES, G], F32, name="b2_sum")
         nc.vector.tensor_tensor(
             out=b2_sum[:],
-            in0=b_sum[:],
+            in0=b0_sum[:],
             in1=bias_ps[:, 0:G].unsqueeze(1).to_broadcast([P, HALVES, G]),
             op=ALU.add,
         )
 
-        peak = sb.tile([P, HALVES, G], F32, name="peak")
-        for h in range(HALVES):
+        out_halves = out.rearrange("(h p) g -> h p g", p=P)
+        for h, queue in enumerate((nc.scalar, nc.sync)):
+            peak = sb.tile([P, G], F32, name="peak%d" % h)
             nc.vector.tensor_reduce(
-                out=peak[:, h, :],
+                out=peak[:],
                 in_=a_ps[h][:].rearrange("p (g r) -> p g r", r=SET),
-                axis=AX,
+                axis=FREE_AXIS,
                 op=ALU.max,
             )
-        res = sb.tile([P, HALVES * G], F32, name="res")
-        nc.vector.scalar_tensor_tensor(
-            out=res[:],
-            in0=b2_sum[:].rearrange("p h g -> p (h g)"),
-            scalar=-1.5 / SET,
-            in1=peak[:].rearrange("p h g -> p (h g)"),
-            op0=ALU.mult,
-            op1=ALU.add,
-        )
-        nc.sync.dma_start(
-            out=out.rearrange("(h p) g -> p h g", p=P),
-            in_=res[:].rearrange("p (h g) -> p h g", g=G),
-        )
+            result = sb.tile([P, G], F32, name="result%d" % h)
+            nc.vector.scalar_tensor_tensor(
+                out=result[:],
+                in0=b2_sum[:, h, :],
+                scalar=-1.5 / SET,
+                in1=peak[:],
+                op0=ALU.mult,
+                op1=ALU.add,
+            )
+            queue.dma_start(out=out_halves[h], in_=result[:])

from contextlib import ExitStack

import concourse.mybir as mybir
from concourse.masks import make_identity

K, T, J, N, L, G = 1024, 1024, 256, 256, 512, 32
FLOPS = 2 * J * N * (K + L)

F32 = mybir.dt.float32
BF16 = mybir.dt.bfloat16
I32 = mybir.dt.int32
U32 = mybir.dt.uint32
U16 = mybir.dt.uint16
U8 = mybir.dt.uint8
E4M3 = mybir.dt.float8_e4m3fn_x4
E5M2 = mybir.dt.float8_e5m2_x4
ALU = mybir.AluOpType
FREE_AXIS = mybir.AxisListType.X

P = 128
PACK = 4
QUADRANT = 32
ROWS = 4
LIST_GROUP = 16
ALIGN = 64
SET = N // G
PASSES = K // (P * PACK)
HALVES = J // P


def load_scale_rows(queue, plane, scales, which):
    passes = scales.shape[0]
    rows = scales.rearrange("z (q r) c -> r q z c", r=ROWS)
    for r in which:
        queue.dma_start(
            out=plane[r:P:QUADRANT, :].bitcast(I32).rearrange("q (z c) -> q z c", z=passes),
            in_=rows[r].bitcast(I32),
        )


def words_by_partition(words):
    return words.rearrange("z p c t -> p z (c t)").bitcast(I32)


def tile_list_rows_owninput_peakofgroups_kernel(
    tc, xt_words, xt_scales, wa_words, wa_scales, sx, wb_words, wb_scales, bi, offs, out
):
    nc = tc.nc
    with ExitStack() as ctx:
        sb = ctx.enter_context(tc.tile_pool(name="sb", bufs=1))
        ps = ctx.enter_context(tc.psum_pool(name="ps", bufs=1))

        offsets = sb.tile([P, J // LIST_GROUP], U16, name="offsets")
        xt_s = sb.tile([P, PASSES * T], U8, name="xt_s", align_bytes=ALIGN)
        xt_w = sb.tile([P, PASSES, T], I32, name="xt_w", align_bytes=ALIGN)
        sx_raw = sb.tile([P, PACK, J], F32, name="sx_raw", align_bytes=ALIGN)
        wa_w = sb.tile([P, PASSES, N], I32, name="wa_w", align_bytes=ALIGN)
        wa_s = sb.tile([P, PASSES * N], U8, name="wa_s", align_bytes=ALIGN)
        wb_w = sb.tile([P, 1, N], I32, name="wb_w", align_bytes=ALIGN)
        wb_s = sb.tile([P, N], U8, name="wb_s", align_bytes=ALIGN)
        bias = sb.tile([G, SET], F32, name="bias")
        bias_sum = sb.tile([P, 1], F32, name="bias_sum")
        ident = sb.tile([P, P], F32, name="ident")

        nc.vector.memset(xt_s[:].bitcast(I32), 0)
        nc.vector.memset(bias_sum[:], 0.0)
        nc.vector.memset(ident[:], 0.0)

        nc.sync.dma_start(offsets[:], offs)
        nc.scalar.dma_start(out=bias[:], in_=bi.rearrange("o (g r) -> (o g) r", r=SET))
        load_scale_rows(nc.gpsimd, wb_s, wb_scales, (2, 3))
        load_scale_rows(nc.gpsimd, wa_s, wa_scales, (3,))
        nc.sync.dma_start(out=sx_raw[:], in_=sx.rearrange("(p t) j -> p t j", t=PACK))
        load_scale_rows(nc.sync, xt_s, xt_scales, range(ROWS))
        nc.sync.dma_start(out=xt_w[:], in_=words_by_partition(xt_words))
        load_scale_rows(nc.sync, wb_s, wb_scales, (0,))
        nc.sync.dma_start(out=wb_w[:], in_=words_by_partition(wb_words))
        load_scale_rows(nc.sync, wb_s, wb_scales, (1,))
        nc.sync.dma_start(out=wa_w[:], in_=words_by_partition(wa_words))
        load_scale_rows(nc.sync, wa_s, wa_scales, (0, 1, 2))
        make_identity(nc, ident[:], nomemset=True)

        nc.vector.tensor_reduce(out=bias_sum[0:G, :], in_=bias[:], axis=FREE_AXIS, op=ALU.add)
        bias_ps = ps.tile([P, P], F32, name="bias_ps")
        nc.tensor.transpose(bias_ps[:], bias_sum[:].to_broadcast([P, P]), ident[:])

        picked_s = [sb.tile([P, J], U8, name="picked_s%d" % z, align_bytes=ALIGN) for z in range(PASSES)]
        for z in range(PASSES):
            nc.vector.tensor_copy(picked_s[z][:], xt_s[:, z * T : (z + 1) * T].indirect(offsets[:]))

        sx_bf = sb.tile([P, J, PACK], BF16, name="sx_bf", align_bytes=ALIGN)
        nc.scalar.copy(out=sx_bf[:], in_=sx_raw[:].rearrange("p t j -> p j t"))
        sx_w = sb.tile([P, J], U32, name="sx_w", align_bytes=ALIGN)
        sx_s = sb.tile([P, J], U8, name="sx_s", align_bytes=ALIGN)
        nc.vector.quantize_mx(
            out=sx_w[:].bitcast(E5M2), scales=sx_s[:], in_=sx_bf[:].rearrange("p j t -> p (j t)")
        )

        picked_w = [sb.tile([P, J], U32, name="picked_w%d" % z, align_bytes=ALIGN) for z in range(PASSES)]
        for z in range(PASSES):
            nc.vector.tensor_copy(picked_w[z][:], xt_w[:, z, :].bitcast(U32).indirect(offsets[:]))

        b_ps = ps.tile([P, HALVES, N], F32, name="b_ps")
        for h in range(HALVES):
            slots = slice(h * P, (h + 1) * P)
            nc.tensor.matmul_mx(
                out=b_ps[:, h, :],
                lhsT=sx_w[:, slots].bitcast(E5M2),
                lhsT_scale=sx_s[:, slots],
                rhs=wb_w[:, 0, :].bitcast(E5M2),
                rhs_scale=wb_s[:],
                start=True,
                stop=True,
            )

        a_ps = [ps.tile([P, N], F32, name="a_ps%d" % h) for h in range(HALVES)]
        for h in range(HALVES):
            slots = slice(h * P, (h + 1) * P)
            for z in range(PASSES):
                nc.tensor.matmul_mx(
                    out=a_ps[h][:],
                    lhsT=picked_w[z][:, slots].bitcast(E4M3),
                    lhsT_scale=picked_s[z][:, slots],
                    rhs=wa_w[:, z, :].bitcast(E5M2),
                    rhs_scale=wa_s[:, z * N : (z + 1) * N],
                    start=(z == 0),
                    stop=(z == PASSES - 1),
                )

        b0_sum = sb.tile([P, HALVES, G], F32, name="b0_sum")
        nc.vector.tensor_reduce(
            out=b0_sum[:].rearrange("p h g -> p (h g)"),
            in_=b_ps[:].rearrange("p h (g r) -> p (h g) r", r=SET),
            axis=FREE_AXIS,
            op=ALU.add,
        )
        b2_sum = sb.tile([P, HALVES, G], F32, name="b2_sum")
        nc.vector.tensor_tensor(
            out=b2_sum[:],
            in0=b0_sum[:],
            in1=bias_ps[:, 0:G].unsqueeze(1).to_broadcast([P, HALVES, G]),
            op=ALU.add,
        )

        out_halves = out.rearrange("(h p) g -> h p g", p=P)
        for h, queue in enumerate((nc.scalar, nc.sync)):
            peak = sb.tile([P, G], F32, name="peak%d" % h)
            nc.vector.tensor_reduce(
                out=peak[:],
                in_=a_ps[h][:].rearrange("p (g r) -> p g r", r=SET),
                axis=FREE_AXIS,
                op=ALU.max,
            )
            result = sb.tile([P, G], F32, name="result%d" % h)
            nc.vector.scalar_tensor_tensor(
                out=result[:],
                in0=b2_sum[:, h, :],
                scalar=-1.5 / SET,
                in1=peak[:],
                op0=ALU.mult,
                op1=ALU.add,
            )
            queue.dma_start(out=out_halves[h], in_=result[:])
